import numpy as np
import ml_dtypes


def mxq(x, axis, fmt="e4m3"):
    dtype, down = {"e4m3": (ml_dtypes.float8_e4m3fn, 7), "e5m2": (ml_dtypes.float8_e5m2, 14)}[fmt]
    v = np.moveaxis(np.asarray(x, np.float32).astype(ml_dtypes.bfloat16).astype(np.float64), axis, -1)
    blocks = v.reshape(v.shape[:-1] + (-1, 32))
    amax = np.abs(blocks).max(-1, keepdims=True)
    byte = np.maximum(np.where(amax > 0, np.frexp(amax)[1] - 1 + 127, 0) - down, 1)
    scale = np.exp2(byte - 127.0)
    codes = (blocks / scale).astype(np.float32).astype(dtype).astype(np.float64)
    return np.moveaxis((codes * scale).reshape(v.shape), -1, axis)


WIDE = False


def mx_kscale(k):
    if not WIDE:
        return np.ones(k)
    levels = np.array([10, -10, 5, -5, 0])
    if k % 512:
        return np.exp2(np.random.permutation(np.resize(levels, k // 32))).repeat(32)
    a = np.empty((k // 512, 16))
    for p in range(k // 512):
        a[p, :8] = np.random.permutation(np.resize(levels, 8))
        for g in range(8):
            far = levels[np.abs(levels - a[p, g]) >= 10]
            a[p, g + 8] = far[np.random.randint(len(far))]
    return np.exp2(a.ravel()).repeat(32)


def f64(x):
    return np.asarray(x).astype(np.float64)


def striped(idx):
    return np.tile(np.asarray(idx).reshape(-1, 16).T, (8, 1)).astype(np.uint16)


def unstriped(offs):
    return offs[:16].T.reshape(-1).astype(np.int64)


E2M1 = np.array([0.0, 0.5, 1.0, 1.5, 2.0, 3.0, 4.0, 6.0, -0.0, -0.5, -1.0, -1.5, -2.0, -3.0, -4.0, -6.0])


def pack_weight(w, fmt):
    k, n = w.shape
    w = f64(np.asarray(w, np.float32).astype(ml_dtypes.bfloat16)).reshape(k // 32, 32, n)
    amax = np.abs(w).max(1)
    if fmt == "e4m3":
        byte = np.frexp(amax)[1] - 1 + 127 - 7
    else:
        mant, ex = np.frexp(amax / 6.0)
        byte = np.where(mant > 0.5, ex, ex - 1) + 127
    byte = np.clip(np.where(amax > 0, byte, 1), 1, 254)
    scaled = (w * np.exp2(127.0 - byte)[:, None, :]).reshape(k, n).astype(np.float32)
    by_word = np.ascontiguousarray(scaled.reshape(k // 512, 128, 4, n).transpose(0, 1, 3, 2))
    if fmt == "e4m3":
        words = by_word.astype(ml_dtypes.float8_e4m3fn).view(np.uint8)
    else:
        c = by_word.astype(ml_dtypes.float4_e2m1fn).view(np.uint8) & 0xF
        words = (c[..., 0::2] | (c[..., 1::2] << 4)).reshape(k // 512, 128, 2 * n)
    return np.ascontiguousarray(words), np.ascontiguousarray(byte.astype(np.uint8).reshape(k // 512, 16, n))


def unpack_weight(words, scales, fmt):
    g, _, n = scales.shape
    words = np.ascontiguousarray(words).reshape(g, 128, n, -1)
    if fmt == "e4m3":
        vals = words.view(ml_dtypes.float8_e4m3fn).astype(np.float64)
    else:
        nib = np.empty((g, 128, n, 4), np.uint8)
        nib[..., 0::2] = words & 0xF
        nib[..., 1::2] = words >> 4
        vals = E2M1[nib]
    vals = vals * np.repeat(np.exp2(scales.astype(np.float64) - 127.0), 8, axis=1)[..., None]
    return vals.transpose(0, 1, 3, 2).reshape(g * 512, n)


def silu(v):
    return v / (1.0 + np.exp(-v))


def bf(x):
    return np.asarray(x, np.float32).astype(ml_dtypes.bfloat16)


def planes(Y):
    r, m = Y.shape
    b = f64(bf(Y)).reshape(r // 32, 32, m)
    amax = np.abs(b).max(1)
    byte = np.clip(np.where(amax > 0, np.frexp(amax)[1] - 1 + 127 - 7, 1), 1, 254)
    codes = (b * np.exp2(127.0 - byte)[:, None, :]).reshape(r, m).astype(np.float32).astype(ml_dtypes.float8_e4m3fn).view(np.uint8)
    words = codes.reshape(r // 512, 128, 4, m).transpose(0, 1, 3, 2)
    return np.ascontiguousarray(words), np.ascontiguousarray(byte.astype(np.uint8).reshape(r // 512, 16, m))


B, N, T, D, NQ = 1, 512, 2048, 512, 256


def setup_inputs():
    n = np.random.standard_normal
    idx = np.random.permutation(T)[:B * N]
    s = mx_kscale(D)[:, None]
    kp = pack_weight(n((D, T)) / s, "e4m3")
    return {
        "qT": (n((B, D, NQ)) * s * (1.00 / np.sqrt(D))).astype(np.float32),
        "k_words": kp[0],
        "k_scales": kp[1],
        "offs": striped(idx),
    }


def reference(qT, k_words, k_scales, offs):
    idx = unstriped(offs)
    pick = lambda x, which: x[:, which].reshape(x.shape[0], B, -1).transpose(1, 0, 2)
    k = unpack_weight(k_words, k_scales, "e4m3")
    kg = pick(k, idx)
    qq = mxq(f64(qT), 1, "e4m3")
    a = kg.transpose(0, 2, 1) @ qq
    y = silu(a)
    Y = y[0]
    words, scales = planes(Y)
    return Y, words, scales

@@ -1,0 +1,111 @@
+from contextlib import ExitStack
+
+import concourse.mybir as mybir
+
+F32 = mybir.dt.float32
+BF16 = mybir.dt.bfloat16
+I32 = mybir.dt.int32
+U32 = mybir.dt.uint32
+U16 = mybir.dt.uint16
+U8 = mybir.dt.uint8
+FP8X4 = mybir.dt.float8_e4m3fn_x4
+SILU = mybir.ActivationFunctionType.Silu
+
+P = 128
+PACK = 4
+SLOTS = 512
+TOKENS = 2048
+QUERIES = 256
+HALF = 128
+FLOPS = 2 * 512 * SLOTS * QUERIES
+
+
+def interleave(copy, dst, src):
+    copy(out=dst.rearrange("p (c i) t -> p c t i", i=4), in_=src.rearrange("p t (c i) -> p c t i", i=4))
+
+
+def tile_attend_plw_silu_topk_kernel(tc, qT, k_words, k_scales, offs, out_0, out_1, out_2):
+    nc = tc.nc
+    halves = QUERIES // HALF
+    with ExitStack() as ctx:
+        keep = ctx.enter_context(tc.tile_pool(name="keep", bufs=1))
+        psum = ctx.enter_context(tc.psum_pool(name="psum", bufs=1))
+
+        offsets = keep.tile([P, SLOTS // 16], U16, name="offsets")
+        pool_words = keep.tile([P, TOKENS], U32, name="pool_words", align_bytes=64)
+        pool_scales = keep.tile([P, TOKENS], U8, name="pool_scales", align_bytes=64)
+        warm = keep.tile([P, 1], F32, name="warm")
+
+        nc.vector.memset(pool_scales[:].bitcast(I32), 0)
+        nc.vector.memset(warm[:], 0.0)
+        nc.sync.dma_start(offsets[:], offs)
+        for quad in range(4):
+            nc.scalar.dma_start(
+                pool_scales[32 * quad : 32 * quad + 4, :].bitcast(I32),
+                k_scales[0, 4 * quad : 4 * quad + 4, :].bitcast(I32),
+            )
+        nc.scalar.activation(warm[:], warm[:], SILU)
+        nc.sync.dma_start(pool_words[:].bitcast(I32), k_words[0].rearrange("p t r -> p (t r)").bitcast(I32))
+        q_rows = qT[0].rearrange("(p j) q -> p j q", j=PACK)
+        q_raw = []
+        for h in range(halves):
+            raw = keep.tile([P, PACK, HALF], F32, name=f"q_raw{h}")
+            nc.sync.dma_start(raw[:], q_rows[:, :, h * HALF : (h + 1) * HALF])
+            q_raw.append(raw)
+
+        listed_scales = keep.tile([P, SLOTS], U8, name="listed_scales", align_bytes=64)
+        key_scales = keep.tile([P, SLOTS], U8, name="key_scales", align_bytes=64)
+        key_words = keep.tile([P, SLOTS], U32, name="key_words", align_bytes=64)
+        nc.vector.tensor_copy(listed_scales[:], pool_scales[:].indirect(offsets[:]))
+        nc.vector.tensor_copy(
+            key_scales[:].rearrange("p (r s) -> p r s", r=PACK),
+            listed_scales[:].rearrange("p (s r) -> p r s", r=PACK),
+        )
+        nc.vector.tensor_copy(key_words[:].rearrange("p (r s) -> p s r", r=PACK), pool_words[:].indirect(offsets[:]))
+
+        q_codes = []
+        q_scales = []
+        for h in range(halves):
+            grouped = keep.tile([P, HALF, PACK], BF16, name=f"q_grouped{h}", align_bytes=64)
+            interleave(nc.scalar.copy, grouped[:], q_raw[h][:])
+            codes = keep.tile([P, HALF], U32, name=f"q_codes{h}", align_bytes=64)
+            scales = keep.tile([P, HALF], U8, name=f"q_scales{h}", align_bytes=64)
+            nc.vector.quantize_mx(out=codes[:].bitcast(FP8X4), scales=scales[:], in_=grouped[:].rearrange("p q j -> p (q j)"))
+            q_codes.append(codes)
+            q_scales.append(scales)
+
+        y_codes = keep.tile([P, QUERIES], U32, name="y_codes", align_bytes=64)
+        y_scales = keep.tile([P, QUERIES], U8, name="y_scales", align_bytes=64)
+        y_rows = out_0.rearrange("(p r) q -> p r q", r=PACK)
+        word_rows = out_1[0].rearrange("p q u -> p (q u)").bitcast(I32)
+        for h in range(halves):
+            cols = slice(h * HALF, (h + 1) * HALF)
+            bank = psum.tile([P, PACK, HALF], F32, name=f"bank{h}")
+            for r in range(PACK):
+                keys = slice(r * P, (r + 1) * P)
+                nc.tensor.matmul_mx(
+                    out=bank[:, r, :],
+                    lhsT=key_words[:, keys].bitcast(FP8X4),
+                    lhsT_scale=key_scales[:, keys],
+                    rhs=q_codes[h][:].bitcast(FP8X4),
+                    rhs_scale=q_scales[h][:],
+                    start=True,
+                    stop=True,
+                )
+            y = keep.tile([P, PACK, HALF], F32, name=f"y{h}")
+            nc.scalar.activation(y[:], bank[:], SILU)
+            nc.sync.dma_start(y_rows[:, :, cols], y[:])
+            y_grouped = keep.tile([P, HALF, PACK], BF16, name=f"y_grouped{h}", align_bytes=64)
+            interleave(nc.vector.tensor_copy, y_grouped[:], y[:])
+            nc.vector.quantize_mx(
+                out=y_codes[:, cols].bitcast(FP8X4),
+                scales=y_scales[:, cols],
+                in_=y_grouped[:].rearrange("p q r -> p (q r)"),
+            )
+            nc.sync.dma_start(word_rows[:, cols], y_codes[:, cols].bitcast(I32))
+        for quad in range(4):
+            queue = nc.scalar if quad < 3 else nc.sync
+            queue.dma_start(
+                out_2[0, 4 * quad : 4 * quad + 4, :].bitcast(I32),
+                y_scales[32 * quad : 32 * quad + 4, :].bitcast(I32),
+            )

@@ -17,6 +17,7 @@ SLOTS = 512
 TOKENS = 2048
 QUERIES = 256
 HALF = 128
+LEAD = 512
 FLOPS = 2 * 512 * SLOTS * QUERIES
 
 
@@ -39,13 +40,16 @@ def tile_attend_plw_silu_topk_kernel(tc, qT, k_words, k_scales, offs, out_0, out
         nc.vector.memset(pool_scales[:].bitcast(I32), 0)
         nc.vector.memset(warm[:], 0.0)
         nc.sync.dma_start(offsets[:], offs)
+        word_cols = k_words[0].rearrange("p t r -> p (t r)").bitcast(I32)
+        nc.sync.dma_start(pool_words[:, :LEAD].bitcast(I32), word_cols[:, :LEAD])
         for quad in range(4):
-            nc.scalar.dma_start(
+            queue = nc.sync if quad % 2 else nc.scalar
+            queue.dma_start(
                 pool_scales[32 * quad : 32 * quad + 4, :].bitcast(I32),
                 k_scales[0, 4 * quad : 4 * quad + 4, :].bitcast(I32),
             )
         nc.scalar.activation(warm[:], warm[:], SILU)
-        nc.sync.dma_start(pool_words[:].bitcast(I32), k_words[0].rearrange("p t r -> p (t r)").bitcast(I32))
+        nc.sync.dma_start(pool_words[:, LEAD:].bitcast(I32), word_cols[:, LEAD:])
         q_rows = qT[0].rearrange("(p j) q -> p j q", j=PACK)
         q_raw = []
         for h in range(halves):
@@ -80,23 +84,25 @@ def tile_attend_plw_silu_topk_kernel(tc, qT, k_words, k_scales, offs, out_0, out
         word_rows = out_1[0].rearrange("p q u -> p (q u)").bitcast(I32)
         for h in range(halves):
             cols = slice(h * HALF, (h + 1) * HALF)
-            bank = psum.tile([P, PACK, HALF], F32, name=f"bank{h}")
-            for r in range(PACK):
-                keys = slice(r * P, (r + 1) * P)
-                nc.tensor.matmul_mx(
-                    out=bank[:, r, :],
-                    lhsT=key_words[:, keys].bitcast(FP8X4),
-                    lhsT_scale=key_scales[:, keys],
-                    rhs=q_codes[h][:].bitcast(FP8X4),
-                    rhs_scale=q_scales[h][:],
-                    start=True,
-                    stop=True,
-                )
             y = keep.tile([P, PACK, HALF], F32, name=f"y{h}")
-            nc.scalar.activation(y[:], bank[:], SILU)
-            nc.sync.dma_start(y_rows[:, :, cols], y[:])
             y_grouped = keep.tile([P, HALF, PACK], BF16, name=f"y_grouped{h}", align_bytes=64)
-            interleave(nc.vector.tensor_copy, y_grouped[:], y[:])
+            for pair in range(PACK // 2):
+                bank = psum.tile([P, 2, HALF], F32, name=f"bank{h}{pair}")
+                for e in range(2):
+                    r = 2 * pair + e
+                    keys = slice(r * P, (r + 1) * P)
+                    nc.tensor.matmul_mx(
+                        out=bank[:, e, :],
+                        lhsT=key_words[:, keys].bitcast(FP8X4),
+                        lhsT_scale=key_scales[:, keys],
+                        rhs=q_codes[h][:].bitcast(FP8X4),
+                        rhs_scale=q_scales[h][:],
+                        start=True,
+                        stop=True,
+                    )
+                nc.scalar.activation(y[:, 2 * pair : 2 * pair + 2, :], bank[:], SILU)
+                interleave(nc.vector.tensor_copy, y_grouped[:, :, 2 * pair : 2 * pair + 2], y[:, 2 * pair : 2 * pair + 2, :])
+            nc.sync.dma_start(y_rows[:, :, cols], y[:])
             nc.vector.quantize_mx(
                 out=y_codes[:, cols].bitcast(FP8X4),
                 scales=y_scales[:, cols],

@@ -60,11 +60,17 @@ def tile_attend_plw_silu_topk_kernel(tc, qT, k_words, k_scales, offs, out_0, out
         listed_scales = keep.tile([P, SLOTS], U8, name="listed_scales", align_bytes=64)
         key_scales = keep.tile([P, SLOTS], U8, name="key_scales", align_bytes=64)
         key_words = keep.tile([P, SLOTS], U32, name="key_words", align_bytes=64)
-        nc.vector.tensor_copy(listed_scales[:], pool_scales[:].indirect(offsets[:]))
-        nc.vector.tensor_copy(
-            key_scales[:].rearrange("p (r s) -> p r s", r=PACK),
-            listed_scales[:].rearrange("p (s r) -> p r s", r=PACK),
-        )
+        half_list = SLOTS // 2
+        for part in range(2):
+            nc.vector.tensor_copy(
+                listed_scales[:, part * half_list : (part + 1) * half_list],
+                pool_scales[:].indirect(offsets[:, part * half_list // 16 : (part + 1) * half_list // 16]),
+            )
+        dealt = key_scales[:].rearrange("p (r s) -> p r s", r=PACK)
+        listed = listed_scales[:].rearrange("p (s r) -> p r s", r=PACK)
+        for part in range(2):
+            rows = slice(part * P // 2, (part + 1) * P // 2)
+            nc.vector.tensor_copy(dealt[:, :, rows], listed[:, :, rows])
         nc.vector.tensor_copy(key_words[:].rearrange("p (r s) -> p s r", r=PACK), pool_words[:].indirect(offsets[:]))
 
         q_codes = []
@@ -80,11 +86,11 @@ def tile_attend_plw_silu_topk_kernel(tc, qT, k_words, k_scales, offs, out_0, out
 
         y_codes = keep.tile([P, QUERIES], U32, name="y_codes", align_bytes=64)
         y_scales = keep.tile([P, QUERIES], U8, name="y_scales", align_bytes=64)
+        y = [keep.tile([P, PACK, HALF], F32, name=f"y{h}") for h in range(halves)]
         y_rows = out_0.rearrange("(p r) q -> p r q", r=PACK)
         word_rows = out_1[0].rearrange("p q u -> p (q u)").bitcast(I32)
         for h in range(halves):
             cols = slice(h * HALF, (h + 1) * HALF)
-            y = keep.tile([P, PACK, HALF], F32, name=f"y{h}")
             y_grouped = keep.tile([P, HALF, PACK], BF16, name=f"y_grouped{h}", align_bytes=64)
             for pair in range(PACK // 2):
                 bank = psum.tile([P, 2, HALF], F32, name=f"bank{h}{pair}")
@@ -100,15 +106,23 @@ def tile_attend_plw_silu_topk_kernel(tc, qT, k_words, k_scales, offs, out_0, out
                         start=True,
                         stop=True,
                     )
-                nc.scalar.activation(y[:, 2 * pair : 2 * pair + 2, :], bank[:], SILU)
-                interleave(nc.vector.tensor_copy, y_grouped[:, :, 2 * pair : 2 * pair + 2], y[:, 2 * pair : 2 * pair + 2, :])
-            nc.sync.dma_start(y_rows[:, :, cols], y[:])
+                places = slice(2 * pair, 2 * pair + 2)
+                if (h, pair) == (halves - 1, PACK // 2 - 1):
+                    nc.scalar.activation(y_grouped[:, :, places], bank[:].rearrange("p e q -> p q e"), SILU)
+                    nc.scalar.activation(y[h][:, places, :], bank[:], SILU)
+                else:
+                    nc.scalar.activation(y[h][:, places, :], bank[:], SILU)
+                    interleave(nc.vector.tensor_copy, y_grouped[:, :, places], y[h][:, places, :])
+                if h == halves - 1:
+                    nc.sync.dma_start(y_rows[:, places, cols], y[h][:, places, :])
+            if h < halves - 1:
+                nc.sync.dma_start(y_rows[:, :, cols], y[h][:])
             nc.vector.quantize_mx(
                 out=y_codes[:, cols].bitcast(FP8X4),
                 scales=y_scales[:, cols],
                 in_=y_grouped[:].rearrange("p q r -> p (q r)"),
             )
-            nc.sync.dma_start(word_rows[:, cols], y_codes[:, cols].bitcast(I32))
+        nc.sync.dma_start(word_rows, y_codes[:].bitcast(I32))
         for quad in range(4):
             queue = nc.scalar if quad < 3 else nc.sync
             queue.dma_start(

@@ -17,7 +17,7 @@ SLOTS = 512
 TOKENS = 2048
 QUERIES = 256
 HALF = 128
-LEAD = 512
+LEAD = 256
 FLOPS = 2 * 512 * SLOTS * QUERIES
 
 
@@ -43,7 +43,7 @@ def tile_attend_plw_silu_topk_kernel(tc, qT, k_words, k_scales, offs, out_0, out
         word_cols = k_words[0].rearrange("p t r -> p (t r)").bitcast(I32)
         nc.sync.dma_start(pool_words[:, :LEAD].bitcast(I32), word_cols[:, :LEAD])
         for quad in range(4):
-            queue = nc.sync if quad % 2 else nc.scalar
+            queue = nc.scalar if quad < 2 else nc.sync
             queue.dma_start(
                 pool_scales[32 * quad : 32 * quad + 4, :].bitcast(I32),
                 k_scales[0, 4 * quad : 4 * quad + 4, :].bitcast(I32),

@@ -17,7 +17,7 @@ SLOTS = 512
 TOKENS = 2048
 QUERIES = 256
 HALF = 128
-LEAD = 256
+LEAD = 128
 FLOPS = 2 * 512 * SLOTS * QUERIES
 
 
@@ -49,7 +49,8 @@ def tile_attend_plw_silu_topk_kernel(tc, qT, k_words, k_scales, offs, out_0, out
                 k_scales[0, 4 * quad : 4 * quad + 4, :].bitcast(I32),
             )
         nc.scalar.activation(warm[:], warm[:], SILU)
-        nc.sync.dma_start(pool_words[:, LEAD:].bitcast(I32), word_cols[:, LEAD:])
+        nc.sync.dma_start(pool_words[:, LEAD : 2 * LEAD].bitcast(I32), word_cols[:, LEAD : 2 * LEAD])
+        nc.sync.dma_start(pool_words[:, 2 * LEAD :].bitcast(I32), word_cols[:, 2 * LEAD :])
         q_rows = qT[0].rearrange("(p j) q -> p j q", j=PACK)
         q_raw = []
         for h in range(halves):

@@ -87,16 +87,18 @@ def tile_attend_plw_silu_topk_kernel(tc, qT, k_words, k_scales, offs, out_0, out
 
         y_codes = keep.tile([P, QUERIES], U32, name="y_codes", align_bytes=64)
         y_scales = keep.tile([P, QUERIES], U8, name="y_scales", align_bytes=64)
-        y = [keep.tile([P, PACK, HALF], F32, name=f"y{h}") for h in range(halves)]
+        y = keep.tile([P, PACK, QUERIES], F32, name="y")
         y_rows = out_0.rearrange("(p r) q -> p r q", r=PACK)
         word_rows = out_1[0].rearrange("p q u -> p (q u)").bitcast(I32)
+        low, high = slice(0, 2), slice(2, 4)
+        pair_order = [[low, high], [high, low]]
         for h in range(halves):
             cols = slice(h * HALF, (h + 1) * HALF)
             y_grouped = keep.tile([P, HALF, PACK], BF16, name=f"y_grouped{h}", align_bytes=64)
-            for pair in range(PACK // 2):
-                bank = psum.tile([P, 2, HALF], F32, name=f"bank{h}{pair}")
+            for n, places in enumerate(pair_order[h]):
+                bank = psum.tile([P, 2, HALF], F32, name=f"bank{h}{n}")
                 for e in range(2):
-                    r = 2 * pair + e
+                    r = places.start + e
                     keys = slice(r * P, (r + 1) * P)
                     nc.tensor.matmul_mx(
                         out=bank[:, e, :],
@@ -107,17 +109,16 @@ def tile_attend_plw_silu_topk_kernel(tc, qT, k_words, k_scales, offs, out_0, out
                         start=True,
                         stop=True,
                     )
-                places = slice(2 * pair, 2 * pair + 2)
-                if (h, pair) == (halves - 1, PACK // 2 - 1):
+                if (h, n) == (halves - 1, 1):
                     nc.scalar.activation(y_grouped[:, :, places], bank[:].rearrange("p e q -> p q e"), SILU)
-                    nc.scalar.activation(y[h][:, places, :], bank[:], SILU)
+                    nc.scalar.activation(y[:, places, cols], bank[:], SILU)
                 else:
-                    nc.scalar.activation(y[h][:, places, :], bank[:], SILU)
-                    interleave(nc.vector.tensor_copy, y_grouped[:, :, places], y[h][:, places, :])
-                if h == halves - 1:
-                    nc.sync.dma_start(y_rows[:, places, cols], y[h][:, places, :])
-            if h < halves - 1:
-                nc.sync.dma_start(y_rows[:, :, cols], y[h][:])
+                    nc.scalar.activation(y[:, places, cols], bank[:], SILU)
+                    interleave(nc.vector.tensor_copy, y_grouped[:, :, places], y[:, places, cols])
+                if places == low:
+                    nc.sync.dma_start(y_rows[:, low, cols], y[:, low, cols])
+                elif h == halves - 1:
+                    nc.sync.dma_start(y_rows[:, high, :], y[:, high, :])
             nc.vector.quantize_mx(
                 out=y_codes[:, cols].bitcast(FP8X4),
                 scales=y_scales[:, cols],

@@ -30,6 +30,7 @@ def tile_attend_plw_silu_topk_kernel(tc, qT, k_words, k_scales, offs, out_0, out
     halves = QUERIES // HALF
     with ExitStack() as ctx:
         keep = ctx.enter_context(tc.tile_pool(name="keep", bufs=1))
+        shared = ctx.enter_context(tc.tile_pool(name="shared", bufs=1))
         psum = ctx.enter_context(tc.psum_pool(name="psum", bufs=1))
 
         offsets = keep.tile([P, SLOTS // 16], U16, name="offsets")
@@ -54,34 +55,37 @@ def tile_attend_plw_silu_topk_kernel(tc, qT, k_words, k_scales, offs, out_0, out
         q_rows = qT[0].rearrange("(p j) q -> p j q", j=PACK)
         q_raw = []
         for h in range(halves):
-            raw = keep.tile([P, PACK, HALF], F32, name=f"q_raw{h}")
+            raw = shared.tile([P, PACK, HALF], F32, name=f"q_raw{h}", offset=h * PACK * HALF * 4, align_bytes=64)
             nc.sync.dma_start(raw[:], q_rows[:, :, h * HALF : (h + 1) * HALF])
             q_raw.append(raw)
 
         listed_scales = keep.tile([P, SLOTS], U8, name="listed_scales", align_bytes=64)
-        key_scales = keep.tile([P, SLOTS], U8, name="key_scales", align_bytes=64)
         key_words = keep.tile([P, SLOTS], U32, name="key_words", align_bytes=64)
-        half_list = SLOTS // 2
-        for part in range(2):
-            nc.vector.tensor_copy(
-                listed_scales[:, part * half_list : (part + 1) * half_list],
-                pool_scales[:].indirect(offsets[:, part * half_list // 16 : (part + 1) * half_list // 16]),
-            )
-        dealt = key_scales[:].rearrange("p (r s) -> p r s", r=PACK)
-        listed = listed_scales[:].rearrange("p (s r) -> p r s", r=PACK)
-        for part in range(2):
-            rows = slice(part * P // 2, (part + 1) * P // 2)
-            nc.vector.tensor_copy(dealt[:, :, rows], listed[:, :, rows])
+        nc.vector.tensor_copy(listed_scales[:], pool_scales[:].indirect(offsets[:]))
         nc.vector.tensor_copy(key_words[:].rearrange("p (r s) -> p s r", r=PACK), pool_words[:].indirect(offsets[:]))
+        listed = listed_scales[:].rearrange("p (s r) -> p r s", r=PACK)
+
+        key_scales = []
+
+        def deal_scales(r):
+            dealt = shared.tile([P, P], U8, name=f"key_scales{r}", offset=r * P, align_bytes=64)
+            nc.vector.tensor_copy(dealt[:], listed[:, r, :])
+            key_scales.append(dealt)
 
         q_codes = []
         q_scales = []
         for h in range(halves):
             grouped = keep.tile([P, HALF, PACK], BF16, name=f"q_grouped{h}", align_bytes=64)
             interleave(nc.scalar.copy, grouped[:], q_raw[h][:])
+            if h == 0:
+                deal_scales(0)
+                deal_scales(1)
             codes = keep.tile([P, HALF], U32, name=f"q_codes{h}", align_bytes=64)
             scales = keep.tile([P, HALF], U8, name=f"q_scales{h}", align_bytes=64)
             nc.vector.quantize_mx(out=codes[:].bitcast(FP8X4), scales=scales[:], in_=grouped[:].rearrange("p q j -> p (q j)"))
+            if h == 0:
+                deal_scales(2)
+                deal_scales(3)
             q_codes.append(codes)
             q_scales.append(scales)
 
@@ -103,7 +107,7 @@ def tile_attend_plw_silu_topk_kernel(tc, qT, k_words, k_scales, offs, out_0, out
                     nc.tensor.matmul_mx(
                         out=bank[:, e, :],
                         lhsT=key_words[:, keys].bitcast(FP8X4),
-                        lhsT_scale=key_scales[:, keys],
+                        lhsT_scale=key_scales[r][:],
                         rhs=q_codes[h][:].bitcast(FP8X4),
                         rhs_scale=q_scales[h][:],
                         start=True,
@@ -126,7 +130,7 @@ def tile_attend_plw_silu_topk_kernel(tc, qT, k_words, k_scales, offs, out_0, out
             )
         nc.sync.dma_start(word_rows, y_codes[:].bitcast(I32))
         for quad in range(4):
-            queue = nc.scalar if quad < 3 else nc.sync
+            queue = nc.scalar if quad < 2 else nc.sync
             queue.dma_start(
                 out_2[0, 4 * quad : 4 * quad + 4, :].bitcast(I32),
                 y_scales[32 * quad : 32 * quad + 4, :].bitcast(I32),

@@ -17,7 +17,8 @@ SLOTS = 512
 TOKENS = 2048
 QUERIES = 256
 HALF = 128
-LEAD = 128
+LEAD = 256
+SPACER = 128
 FLOPS = 2 * 512 * SLOTS * QUERIES
 
 
@@ -40,9 +41,9 @@ def tile_attend_plw_silu_topk_kernel(tc, qT, k_words, k_scales, offs, out_0, out
 
         nc.vector.memset(pool_scales[:].bitcast(I32), 0)
         nc.vector.memset(warm[:], 0.0)
-        nc.sync.dma_start(offsets[:], offs)
         word_cols = k_words[0].rearrange("p t r -> p (t r)").bitcast(I32)
         nc.sync.dma_start(pool_words[:, :LEAD].bitcast(I32), word_cols[:, :LEAD])
+        nc.sync.dma_start(offsets[:], offs)
         for quad in range(4):
             queue = nc.scalar if quad < 2 else nc.sync
             queue.dma_start(
@@ -50,8 +51,8 @@ def tile_attend_plw_silu_topk_kernel(tc, qT, k_words, k_scales, offs, out_0, out
                 k_scales[0, 4 * quad : 4 * quad + 4, :].bitcast(I32),
             )
         nc.scalar.activation(warm[:], warm[:], SILU)
-        nc.sync.dma_start(pool_words[:, LEAD : 2 * LEAD].bitcast(I32), word_cols[:, LEAD : 2 * LEAD])
-        nc.sync.dma_start(pool_words[:, 2 * LEAD :].bitcast(I32), word_cols[:, 2 * LEAD :])
+        nc.sync.dma_start(pool_words[:, LEAD : LEAD + SPACER].bitcast(I32), word_cols[:, LEAD : LEAD + SPACER])
+        nc.sync.dma_start(pool_words[:, LEAD + SPACER :].bitcast(I32), word_cols[:, LEAD + SPACER :])
         q_rows = qT[0].rearrange("(p j) q -> p j q", j=PACK)
         q_raw = []
         for h in range(halves):

@@ -17,8 +17,8 @@ SLOTS = 512
 TOKENS = 2048
 QUERIES = 256
 HALF = 128
-LEAD = 256
-SPACER = 128
+ROWS = 16
+PARKED = P - ROWS
 FLOPS = 2 * 512 * SLOTS * QUERIES
 
 
@@ -31,7 +31,6 @@ def tile_attend_plw_silu_topk_kernel(tc, qT, k_words, k_scales, offs, out_0, out
     halves = QUERIES // HALF
     with ExitStack() as ctx:
         keep = ctx.enter_context(tc.tile_pool(name="keep", bufs=1))
-        shared = ctx.enter_context(tc.tile_pool(name="shared", bufs=1))
         psum = ctx.enter_context(tc.psum_pool(name="psum", bufs=1))
 
         offsets = keep.tile([P, SLOTS // 16], U16, name="offsets")
@@ -39,54 +38,47 @@ def tile_attend_plw_silu_topk_kernel(tc, qT, k_words, k_scales, offs, out_0, out
         pool_scales = keep.tile([P, TOKENS], U8, name="pool_scales", align_bytes=64)
         warm = keep.tile([P, 1], F32, name="warm")
 
-        nc.vector.memset(pool_scales[:].bitcast(I32), 0)
-        nc.vector.memset(warm[:], 0.0)
-        word_cols = k_words[0].rearrange("p t r -> p (t r)").bitcast(I32)
-        nc.sync.dma_start(pool_words[:, :LEAD].bitcast(I32), word_cols[:, :LEAD])
+        key_scales = keep.tile([P, SLOTS], U8, name="key_scales", align_bytes=64)
+
+        nc.scalar.dma_start(pool_scales[PARKED:, :].bitcast(I32), k_scales[0].bitcast(I32))
         nc.sync.dma_start(offsets[:], offs)
-        for quad in range(4):
-            queue = nc.scalar if quad < 2 else nc.sync
-            queue.dma_start(
-                pool_scales[32 * quad : 32 * quad + 4, :].bitcast(I32),
-                k_scales[0, 4 * quad : 4 * quad + 4, :].bitcast(I32),
-            )
+        word_cols = k_words[0].rearrange("p t r -> p (t r)").bitcast(I32)
+        nc.sync.dma_start(pool_words[:].bitcast(I32), word_cols)
+        nc.vector.memset(warm[:], 0.0)
         nc.scalar.activation(warm[:], warm[:], SILU)
-        nc.sync.dma_start(pool_words[:, LEAD : LEAD + SPACER].bitcast(I32), word_cols[:, LEAD : LEAD + SPACER])
-        nc.sync.dma_start(pool_words[:, LEAD + SPACER :].bitcast(I32), word_cols[:, LEAD + SPACER :])
+        nc.vector.memset(pool_scales[:PARKED, :].bitcast(I32), 0)
+        nc.vector.memset(key_scales[:].bitcast(I32), 0)
         q_rows = qT[0].rearrange("(p j) q -> p j q", j=PACK)
         q_raw = []
         for h in range(halves):
-            raw = shared.tile([P, PACK, HALF], F32, name=f"q_raw{h}", offset=h * PACK * HALF * 4, align_bytes=64)
+            raw = keep.tile([P, PACK, HALF], F32, name=f"q_raw{h}", align_bytes=64)
             nc.sync.dma_start(raw[:], q_rows[:, :, h * HALF : (h + 1) * HALF])
             q_raw.append(raw)
 
         listed_scales = keep.tile([P, SLOTS], U8, name="listed_scales", align_bytes=64)
+        dealt_scales = keep.tile([P, SLOTS], U8, name="dealt_scales", align_bytes=64)
         key_words = keep.tile([P, SLOTS], U32, name="key_words", align_bytes=64)
         nc.vector.tensor_copy(listed_scales[:], pool_scales[:].indirect(offsets[:]))
+        nc.vector.tensor_copy(
+            dealt_scales[:].rearrange("p (r c i) -> p c r i", r=PACK, i=4),
+            listed_scales[:].rearrange("p (c i r) -> p c r i", r=PACK, i=4),
+        )
+        for quad in range(4):
+            queue = nc.scalar if quad < 2 else nc.sync
+            queue.dma_start(
+                key_scales[32 * quad : 32 * quad + 4, :].bitcast(I32),
+                dealt_scales[PARKED + 4 * quad : PARKED + 4 * quad + 4, :].bitcast(I32),
+            )
         nc.vector.tensor_copy(key_words[:].rearrange("p (r s) -> p s r", r=PACK), pool_words[:].indirect(offsets[:]))
-        listed = listed_scales[:].rearrange("p (s r) -> p r s", r=PACK)
-
-        key_scales = []
-
-        def deal_scales(r):
-            dealt = shared.tile([P, P], U8, name=f"key_scales{r}", offset=r * P, align_bytes=64)
-            nc.vector.tensor_copy(dealt[:], listed[:, r, :])
-            key_scales.append(dealt)
 
         q_codes = []
         q_scales = []
         for h in range(halves):
             grouped = keep.tile([P, HALF, PACK], BF16, name=f"q_grouped{h}", align_bytes=64)
             interleave(nc.scalar.copy, grouped[:], q_raw[h][:])
-            if h == 0:
-                deal_scales(0)
-                deal_scales(1)
             codes = keep.tile([P, HALF], U32, name=f"q_codes{h}", align_bytes=64)
             scales = keep.tile([P, HALF], U8, name=f"q_scales{h}", align_bytes=64)
             nc.vector.quantize_mx(out=codes[:].bitcast(FP8X4), scales=scales[:], in_=grouped[:].rearrange("p q j -> p (q j)"))
-            if h == 0:
-                deal_scales(2)
-                deal_scales(3)
             q_codes.append(codes)
             q_scales.append(scales)
 
@@ -108,7 +100,7 @@ def tile_attend_plw_silu_topk_kernel(tc, qT, k_words, k_scales, offs, out_0, out
                     nc.tensor.matmul_mx(
                         out=bank[:, e, :],
                         lhsT=key_words[:, keys].bitcast(FP8X4),
-                        lhsT_scale=key_scales[r][:],
+                        lhsT_scale=key_scales[:, keys],
                         rhs=q_codes[h][:].bitcast(FP8X4),
                         rhs_scale=q_scales[h][:],
                         start=True,

@@ -17,6 +17,7 @@ SLOTS = 512
 TOKENS = 2048
 QUERIES = 256
 HALF = 128
+SHARE = 64
 ROWS = 16
 PARKED = P - ROWS
 FLOPS = 2 * 512 * SLOTS * QUERIES
@@ -49,11 +50,14 @@ def tile_attend_plw_silu_topk_kernel(tc, qT, k_words, k_scales, offs, out_0, out
         nc.vector.memset(pool_scales[:PARKED, :].bitcast(I32), 0)
         nc.vector.memset(key_scales[:].bitcast(I32), 0)
         q_rows = qT[0].rearrange("(p j) q -> p j q", j=PACK)
-        q_raw = []
-        for h in range(halves):
-            raw = keep.tile([P, PACK, HALF], F32, name=f"q_raw{h}", align_bytes=64)
-            nc.sync.dma_start(raw[:], q_rows[:, :, h * HALF : (h + 1) * HALF])
-            q_raw.append(raw)
+        low, high = slice(0, 2), slice(2, 4)
+        first_raw = []
+        for n, rows in enumerate((low, high)):
+            raw = keep.tile([P, 2, HALF], F32, name=f"first_raw{n}", align_bytes=64)
+            nc.sync.dma_start(raw[:], q_rows[:, rows, :HALF])
+            first_raw.append(raw)
+        second_raw = keep.tile([P, PACK, HALF], F32, name="second_raw", align_bytes=64)
+        nc.sync.dma_start(second_raw[:], q_rows[:, :, HALF:])
 
         listed_scales = keep.tile([P, SLOTS], U8, name="listed_scales", align_bytes=64)
         dealt_scales = keep.tile([P, SLOTS], U8, name="dealt_scales", align_bytes=64)
@@ -75,7 +79,12 @@ def tile_attend_plw_silu_topk_kernel(tc, qT, k_words, k_scales, offs, out_0, out
         q_scales = []
         for h in range(halves):
             grouped = keep.tile([P, HALF, PACK], BF16, name=f"q_grouped{h}", align_bytes=64)
-            interleave(nc.scalar.copy, grouped[:], q_raw[h][:])
+            if h == 0:
+                interleave(nc.scalar.copy, grouped[:, :, low], first_raw[0][:])
+                interleave(nc.scalar.copy, grouped[:, :, high], first_raw[1][:])
+            else:
+                interleave(nc.scalar.copy, grouped[:, :SHARE, :], second_raw[:, :, :SHARE])
+                interleave(nc.vector.tensor_copy, grouped[:, SHARE:, :], second_raw[:, :, SHARE:])
             codes = keep.tile([P, HALF], U32, name=f"q_codes{h}", align_bytes=64)
             scales = keep.tile([P, HALF], U8, name=f"q_scales{h}", align_bytes=64)
             nc.vector.quantize_mx(out=codes[:].bitcast(FP8X4), scales=scales[:], in_=grouped[:].rearrange("p q j -> p (q j)"))
@@ -87,7 +96,6 @@ def tile_attend_plw_silu_topk_kernel(tc, qT, k_words, k_scales, offs, out_0, out
         y = keep.tile([P, PACK, QUERIES], F32, name="y")
         y_rows = out_0.rearrange("(p r) q -> p r q", r=PACK)
         word_rows = out_1[0].rearrange("p q u -> p (q u)").bitcast(I32)
-        low, high = slice(0, 2), slice(2, 4)
         pair_order = [[low, high], [high, low]]
         for h in range(halves):
             cols = slice(h * HALF, (h + 1) * HALF)

@@ -32,11 +32,13 @@ def tile_attend_plw_silu_topk_kernel(tc, qT, k_words, k_scales, offs, out_0, out
     halves = QUERIES // HALF
     with ExitStack() as ctx:
         keep = ctx.enter_context(tc.tile_pool(name="keep", bufs=1))
+        shared = ctx.enter_context(tc.tile_pool(name="shared", bufs=1))
+        rounded = ctx.enter_context(tc.tile_pool(name="rounded", bufs=1))
         psum = ctx.enter_context(tc.psum_pool(name="psum", bufs=1))
 
         offsets = keep.tile([P, SLOTS // 16], U16, name="offsets")
         pool_words = keep.tile([P, TOKENS], U32, name="pool_words", align_bytes=64)
-        pool_scales = keep.tile([P, TOKENS], U8, name="pool_scales", align_bytes=64)
+        pool_scales = shared.tile([P, TOKENS], U8, name="pool_scales", offset=0, align_bytes=64)
         warm = keep.tile([P, 1], F32, name="warm")
 
         key_scales = keep.tile([P, SLOTS], U8, name="key_scales", align_bytes=64)
@@ -53,43 +55,53 @@ def tile_attend_plw_silu_topk_kernel(tc, qT, k_words, k_scales, offs, out_0, out
         low, high = slice(0, 2), slice(2, 4)
         first_raw = []
         for n, rows in enumerate((low, high)):
-            raw = keep.tile([P, 2, HALF], F32, name=f"first_raw{n}", align_bytes=64)
+            raw = rounded.tile([P, 2, HALF], F32, name=f"first_raw{n}", offset=1024 * (n + 1), align_bytes=64)
             nc.sync.dma_start(raw[:], q_rows[:, rows, :HALF])
             first_raw.append(raw)
-        second_raw = keep.tile([P, PACK, HALF], F32, name="second_raw", align_bytes=64)
-        nc.sync.dma_start(second_raw[:], q_rows[:, :, HALF:])
 
         listed_scales = keep.tile([P, SLOTS], U8, name="listed_scales", align_bytes=64)
         dealt_scales = keep.tile([P, SLOTS], U8, name="dealt_scales", align_bytes=64)
         key_words = keep.tile([P, SLOTS], U32, name="key_words", align_bytes=64)
-        nc.vector.tensor_copy(listed_scales[:], pool_scales[:].indirect(offsets[:]))
-        nc.vector.tensor_copy(
-            dealt_scales[:].rearrange("p (r c i) -> p c r i", r=PACK, i=4),
-            listed_scales[:].rearrange("p (c i r) -> p c r i", r=PACK, i=4),
-        )
+        half_list = SLOTS // 2
+        for part in range(2):
+            nc.vector.tensor_copy(
+                listed_scales[:, part * half_list : (part + 1) * half_list],
+                pool_scales[:].indirect(offsets[:, part * half_list // 16 : (part + 1) * half_list // 16]),
+            )
+        second_raw = shared.tile([P, PACK, HALF], F32, name="second_raw", offset=0, align_bytes=64)
+        nc.scalar.dma_start(second_raw[:], q_rows[:, :, HALF:])
+        dealt_view = dealt_scales[:].rearrange("p (r s) -> p r s", r=PACK)
+        for part in range(2):
+            nc.vector.tensor_copy(
+                dealt_view[:, :, part * half_list // PACK : (part + 1) * half_list // PACK],
+                listed_scales[:, part * half_list : (part + 1) * half_list].rearrange("p (s r) -> p r s", r=PACK),
+            )
         for quad in range(4):
-            queue = nc.scalar if quad < 2 else nc.sync
-            queue.dma_start(
+            nc.sync.dma_start(
                 key_scales[32 * quad : 32 * quad + 4, :].bitcast(I32),
                 dealt_scales[PARKED + 4 * quad : PARKED + 4 * quad + 4, :].bitcast(I32),
             )
         nc.vector.tensor_copy(key_words[:].rearrange("p (r s) -> p s r", r=PACK), pool_words[:].indirect(offsets[:]))
 
-        q_codes = []
-        q_scales = []
-        for h in range(halves):
-            grouped = keep.tile([P, HALF, PACK], BF16, name=f"q_grouped{h}", align_bytes=64)
-            if h == 0:
-                interleave(nc.scalar.copy, grouped[:, :, low], first_raw[0][:])
-                interleave(nc.scalar.copy, grouped[:, :, high], first_raw[1][:])
-            else:
-                interleave(nc.scalar.copy, grouped[:, :SHARE, :], second_raw[:, :, :SHARE])
-                interleave(nc.vector.tensor_copy, grouped[:, SHARE:, :], second_raw[:, :, SHARE:])
-            codes = keep.tile([P, HALF], U32, name=f"q_codes{h}", align_bytes=64)
-            scales = keep.tile([P, HALF], U8, name=f"q_scales{h}", align_bytes=64)
-            nc.vector.quantize_mx(out=codes[:].bitcast(FP8X4), scales=scales[:], in_=grouped[:].rearrange("p q j -> p (q j)"))
-            q_codes.append(codes)
-            q_scales.append(scales)
+        q_codes = [
+            keep.tile([P, HALF], U32, name="q_codes0", align_bytes=64),
+            rounded.tile([P, HALF], U32, name="q_codes1", offset=SHARE * PACK * 2, align_bytes=64),
+        ]
+        q_scales = [keep.tile([P, HALF], U8, name=f"q_scales{h}", align_bytes=64) for h in range(halves)]
+        first_grouped = rounded.tile([P, HALF, PACK], BF16, name="first_grouped", offset=0, align_bytes=64)
+        interleave(nc.scalar.copy, first_grouped[:, :, low], first_raw[0][:])
+        interleave(nc.scalar.copy, first_grouped[:, :, high], first_raw[1][:])
+        nc.vector.quantize_mx(
+            out=q_codes[0][:].bitcast(FP8X4), scales=q_scales[0][:], in_=first_grouped[:].rearrange("p q j -> p (q j)")
+        )
+        by_scalar = rounded.tile([P, SHARE, PACK], BF16, name="by_scalar", offset=2048, align_bytes=64)
+        by_vector = rounded.tile([P, SHARE, PACK], BF16, name="by_vector", offset=0, align_bytes=64)
+        interleave(nc.vector.tensor_copy, by_vector[:], second_raw[:, :, SHARE:])
+        interleave(nc.scalar.copy, by_scalar[:], second_raw[:, :, :SHARE])
+        for grouped, cols in ((by_scalar, slice(0, SHARE)), (by_vector, slice(SHARE, HALF))):
+            nc.vector.quantize_mx(
+                out=q_codes[1][:, cols].bitcast(FP8X4), scales=q_scales[1][:, cols], in_=grouped[:].rearrange("p q j -> p (q j)")
+            )
 
         y_codes = keep.tile([P, QUERIES], U32, name="y_codes", align_bytes=64)
         y_scales = keep.tile([P, QUERIES], U8, name="y_scales", align_bytes=64)

@@ -90,7 +90,15 @@ def tile_attend_plw_silu_topk_kernel(tc, qT, k_words, k_scales, offs, out_0, out
         q_scales = [keep.tile([P, HALF], U8, name=f"q_scales{h}", align_bytes=64) for h in range(halves)]
         first_grouped = rounded.tile([P, HALF, PACK], BF16, name="first_grouped", offset=0, align_bytes=64)
         interleave(nc.scalar.copy, first_grouped[:, :, low], first_raw[0][:])
-        interleave(nc.scalar.copy, first_grouped[:, :, high], first_raw[1][:])
+        interleave(nc.scalar.copy, first_grouped[:, :SHARE, high], first_raw[1][:, :, :SHARE])
+        nc.gpsimd.tensor_scalar(
+            out=first_grouped[:, SHARE:, high],
+            in0=first_raw[1][:, :, SHARE:].rearrange("p t c -> p c t"),
+            scalar1=1.0,
+            scalar2=0.0,
+            op0=mybir.AluOpType.mult,
+            op1=mybir.AluOpType.add,
+        )
         nc.vector.quantize_mx(
             out=q_codes[0][:].bitcast(FP8X4), scales=q_scales[0][:], in_=first_grouped[:].rearrange("p q j -> p (q j)")
         )

@@ -18,6 +18,7 @@ TOKENS = 2048
 QUERIES = 256
 HALF = 128
 SHARE = 64
+SCALAR_COLS = 80
 ROWS = 16
 PARKED = P - ROWS
 FLOPS = 2 * 512 * SLOTS * QUERIES
@@ -69,7 +70,8 @@ def tile_attend_plw_silu_topk_kernel(tc, qT, k_words, k_scales, offs, out_0, out
                 pool_scales[:].indirect(offsets[:, part * half_list // 16 : (part + 1) * half_list // 16]),
             )
         second_raw = shared.tile([P, PACK, HALF], F32, name="second_raw", offset=0, align_bytes=64)
-        nc.scalar.dma_start(second_raw[:], q_rows[:, :, HALF:])
+        for rows in (low, high):
+            nc.scalar.dma_start(second_raw[:, rows, :], q_rows[:, rows, HALF:])
         dealt_view = dealt_scales[:].rearrange("p (r s) -> p r s", r=PACK)
         for part in range(2):
             nc.vector.tensor_copy(
@@ -89,23 +91,24 @@ def tile_attend_plw_silu_topk_kernel(tc, qT, k_words, k_scales, offs, out_0, out
         ]
         q_scales = [keep.tile([P, HALF], U8, name=f"q_scales{h}", align_bytes=64) for h in range(halves)]
         first_grouped = rounded.tile([P, HALF, PACK], BF16, name="first_grouped", offset=0, align_bytes=64)
-        interleave(nc.scalar.copy, first_grouped[:, :, low], first_raw[0][:])
-        interleave(nc.scalar.copy, first_grouped[:, :SHARE, high], first_raw[1][:, :, :SHARE])
-        nc.gpsimd.tensor_scalar(
-            out=first_grouped[:, SHARE:, high],
-            in0=first_raw[1][:, :, SHARE:].rearrange("p t c -> p c t"),
-            scalar1=1.0,
-            scalar2=0.0,
-            op0=mybir.AluOpType.mult,
-            op1=mybir.AluOpType.add,
-        )
+        for rows, raw in zip((low, high), first_raw):
+            interleave(nc.scalar.copy, first_grouped[:, :SCALAR_COLS, rows], raw[:, :, :SCALAR_COLS])
+            nc.gpsimd.tensor_scalar(
+                out=first_grouped[:, SCALAR_COLS:, rows],
+                in0=raw[:, :, SCALAR_COLS:].rearrange("p t c -> p c t"),
+                scalar1=1.0,
+                scalar2=0.0,
+                op0=mybir.AluOpType.mult,
+                op1=mybir.AluOpType.add,
+            )
         nc.vector.quantize_mx(
             out=q_codes[0][:].bitcast(FP8X4), scales=q_scales[0][:], in_=first_grouped[:].rearrange("p q j -> p (q j)")
         )
         by_scalar = rounded.tile([P, SHARE, PACK], BF16, name="by_scalar", offset=2048, align_bytes=64)
         by_vector = rounded.tile([P, SHARE, PACK], BF16, name="by_vector", offset=0, align_bytes=64)
         interleave(nc.vector.tensor_copy, by_vector[:], second_raw[:, :, SHARE:])
-        interleave(nc.scalar.copy, by_scalar[:], second_raw[:, :, :SHARE])
+        for rows in (low, high):
+            interleave(nc.scalar.copy, by_scalar[:, :, rows], second_raw[:, rows, :SHARE])
         for grouped, cols in ((by_scalar, slice(0, SHARE)), (by_vector, slice(SHARE, HALF))):
             nc.vector.quantize_mx(
                 out=q_codes[1][:, cols].bitcast(FP8X4), scales=q_scales[1][:, cols], in_=grouped[:].rearrange("p q j -> p (q j)")

@@ -154,7 +154,7 @@ def tile_attend_plw_silu_topk_kernel(tc, qT, k_words, k_scales, offs, out_0, out
             )
         nc.sync.dma_start(word_rows, y_codes[:].bitcast(I32))
         for quad in range(4):
-            queue = nc.scalar if quad < 2 else nc.sync
+            queue = nc.scalar if quad < 3 else nc.sync
             queue.dma_start(
                 out_2[0, 4 * quad : 4 * quad + 4, :].bitcast(I32),
                 y_scales[32 * quad : 32 * quad + 4, :].bitcast(I32),

@@ -60,24 +60,12 @@ def tile_attend_plw_silu_topk_kernel(tc, qT, k_words, k_scales, offs, out_0, out
             nc.sync.dma_start(raw[:], q_rows[:, rows, :HALF])
             first_raw.append(raw)
 
-        listed_scales = keep.tile([P, SLOTS], U8, name="listed_scales", align_bytes=64)
         dealt_scales = keep.tile([P, SLOTS], U8, name="dealt_scales", align_bytes=64)
         key_words = keep.tile([P, SLOTS], U32, name="key_words", align_bytes=64)
-        half_list = SLOTS // 2
-        for part in range(2):
-            nc.vector.tensor_copy(
-                listed_scales[:, part * half_list : (part + 1) * half_list],
-                pool_scales[:].indirect(offsets[:, part * half_list // 16 : (part + 1) * half_list // 16]),
-            )
+        nc.vector.tensor_copy(dealt_scales[:].rearrange("p (r s) -> p s r", r=PACK), pool_scales[:].indirect(offsets[:]))
         second_raw = shared.tile([P, PACK, HALF], F32, name="second_raw", offset=0, align_bytes=64)
         for rows in (low, high):
             nc.scalar.dma_start(second_raw[:, rows, :], q_rows[:, rows, HALF:])
-        dealt_view = dealt_scales[:].rearrange("p (r s) -> p r s", r=PACK)
-        for part in range(2):
-            nc.vector.tensor_copy(
-                dealt_view[:, :, part * half_list // PACK : (part + 1) * half_list // PACK],
-                listed_scales[:, part * half_list : (part + 1) * half_list].rearrange("p (s r) -> p r s", r=PACK),
-            )
         for quad in range(4):
             nc.sync.dma_start(
                 key_scales[32 * quad : 32 * quad + 4, :].bitcast(I32),

@@ -18,7 +18,7 @@ TOKENS = 2048
 QUERIES = 256
 HALF = 128
 SHARE = 64
-SCALAR_COLS = 80
+SCALAR_COLS = 64
 ROWS = 16
 PARKED = P - ROWS
 FLOPS = 2 * 512 * SLOTS * QUERIES

@@ -38,11 +38,11 @@ def tile_attend_plw_silu_topk_kernel(tc, qT, k_words, k_scales, offs, out_0, out
         psum = ctx.enter_context(tc.psum_pool(name="psum", bufs=1))
 
         offsets = keep.tile([P, SLOTS // 16], U16, name="offsets")
-        pool_words = keep.tile([P, TOKENS], U32, name="pool_words", align_bytes=64)
-        pool_scales = shared.tile([P, TOKENS], U8, name="pool_scales", offset=0, align_bytes=64)
+        pool_words = keep.tile([P, TOKENS], U32, name="pool_words", align_bytes=256)
+        pool_scales = shared.tile([P, TOKENS], U8, name="pool_scales", offset=0, align_bytes=256)
         warm = keep.tile([P, 1], F32, name="warm")
 
-        key_scales = keep.tile([P, SLOTS], U8, name="key_scales", align_bytes=64)
+        key_scales = keep.tile([P, SLOTS], U8, name="key_scales", align_bytes=256)
 
         nc.scalar.dma_start(pool_scales[PARKED:, :].bitcast(I32), k_scales[0].bitcast(I32))
         nc.sync.dma_start(offsets[:], offs)
@@ -56,14 +56,14 @@ def tile_attend_plw_silu_topk_kernel(tc, qT, k_words, k_scales, offs, out_0, out
         low, high = slice(0, 2), slice(2, 4)
         first_raw = []
         for n, rows in enumerate((low, high)):
-            raw = rounded.tile([P, 2, HALF], F32, name=f"first_raw{n}", offset=1024 * (n + 1), align_bytes=64)
+            raw = rounded.tile([P, 2, HALF], F32, name=f"first_raw{n}", offset=1024 * (n + 1), align_bytes=256)
             nc.sync.dma_start(raw[:], q_rows[:, rows, :HALF])
             first_raw.append(raw)
 
-        dealt_scales = keep.tile([P, SLOTS], U8, name="dealt_scales", align_bytes=64)
-        key_words = keep.tile([P, SLOTS], U32, name="key_words", align_bytes=64)
+        dealt_scales = keep.tile([P, SLOTS], U8, name="dealt_scales", align_bytes=256)
+        key_words = keep.tile([P, SLOTS], U32, name="key_words", align_bytes=256)
         nc.vector.tensor_copy(dealt_scales[:].rearrange("p (r s) -> p s r", r=PACK), pool_scales[:].indirect(offsets[:]))
-        second_raw = shared.tile([P, PACK, HALF], F32, name="second_raw", offset=0, align_bytes=64)
+        second_raw = shared.tile([P, PACK, HALF], F32, name="second_raw", offset=0, align_bytes=256)
         for rows in (low, high):
             nc.scalar.dma_start(second_raw[:, rows, :], q_rows[:, rows, HALF:])
         for quad in range(4):
@@ -74,11 +74,11 @@ def tile_attend_plw_silu_topk_kernel(tc, qT, k_words, k_scales, offs, out_0, out
         nc.vector.tensor_copy(key_words[:].rearrange("p (r s) -> p s r", r=PACK), pool_words[:].indirect(offsets[:]))
 
         q_codes = [
-            keep.tile([P, HALF], U32, name="q_codes0", align_bytes=64),
-            rounded.tile([P, HALF], U32, name="q_codes1", offset=SHARE * PACK * 2, align_bytes=64),
+            keep.tile([P, HALF], U32, name="q_codes0", align_bytes=256),
+            rounded.tile([P, HALF], U32, name="q_codes1", offset=SHARE * PACK * 2, align_bytes=256),
         ]
-        q_scales = [keep.tile([P, HALF], U8, name=f"q_scales{h}", align_bytes=64) for h in range(halves)]
-        first_grouped = rounded.tile([P, HALF, PACK], BF16, name="first_grouped", offset=0, align_bytes=64)
+        q_scales = [keep.tile([P, HALF], U8, name=f"q_scales{h}", align_bytes=256) for h in range(halves)]
+        first_grouped = rounded.tile([P, HALF, PACK], BF16, name="first_grouped", offset=0, align_bytes=256)
         for rows, raw in zip((low, high), first_raw):
             interleave(nc.scalar.copy, first_grouped[:, :SCALAR_COLS, rows], raw[:, :, :SCALAR_COLS])
             nc.gpsimd.tensor_scalar(
@@ -92,8 +92,8 @@ def tile_attend_plw_silu_topk_kernel(tc, qT, k_words, k_scales, offs, out_0, out
         nc.vector.quantize_mx(
             out=q_codes[0][:].bitcast(FP8X4), scales=q_scales[0][:], in_=first_grouped[:].rearrange("p q j -> p (q j)")
         )
-        by_scalar = rounded.tile([P, SHARE, PACK], BF16, name="by_scalar", offset=2048, align_bytes=64)
-        by_vector = rounded.tile([P, SHARE, PACK], BF16, name="by_vector", offset=0, align_bytes=64)
+        by_scalar = rounded.tile([P, SHARE, PACK], BF16, name="by_scalar", offset=2048, align_bytes=256)
+        by_vector = rounded.tile([P, SHARE, PACK], BF16, name="by_vector", offset=0, align_bytes=256)
         interleave(nc.vector.tensor_copy, by_vector[:], second_raw[:, :, SHARE:])
         for rows in (low, high):
             interleave(nc.scalar.copy, by_scalar[:, :, rows], second_raw[:, rows, :SHARE])
@@ -102,15 +102,15 @@ def tile_attend_plw_silu_topk_kernel(tc, qT, k_words, k_scales, offs, out_0, out
                 out=q_codes[1][:, cols].bitcast(FP8X4), scales=q_scales[1][:, cols], in_=grouped[:].rearrange("p q j -> p (q j)")
             )
 
-        y_codes = keep.tile([P, QUERIES], U32, name="y_codes", align_bytes=64)
-        y_scales = keep.tile([P, QUERIES], U8, name="y_scales", align_bytes=64)
-        y = keep.tile([P, PACK, QUERIES], F32, name="y")
+        y_codes = keep.tile([P, QUERIES], U32, name="y_codes", align_bytes=256)
+        y_scales = keep.tile([P, QUERIES], U8, name="y_scales", align_bytes=256)
+        y = keep.tile([P, PACK, QUERIES], F32, name="y", align_bytes=256)
         y_rows = out_0.rearrange("(p r) q -> p r q", r=PACK)
         word_rows = out_1[0].rearrange("p q u -> p (q u)").bitcast(I32)
         pair_order = [[low, high], [high, low]]
         for h in range(halves):
             cols = slice(h * HALF, (h + 1) * HALF)
-            y_grouped = keep.tile([P, HALF, PACK], BF16, name=f"y_grouped{h}", align_bytes=64)
+            y_grouped = keep.tile([P, HALF, PACK], BF16, name=f"y_grouped{h}", align_bytes=256)
             for n, places in enumerate(pair_order[h]):
                 bank = psum.tile([P, 2, HALF], F32, name=f"bank{h}{n}")
                 for e in range(2):

@@ -97,7 +97,7 @@ def tile_attend_plw_silu_topk_kernel(tc, qT, k_words, k_scales, offs, out_0, out
         interleave(nc.vector.tensor_copy, by_vector[:], second_raw[:, :, SHARE:])
         for rows in (low, high):
             interleave(nc.scalar.copy, by_scalar[:, :, rows], second_raw[:, rows, :SHARE])
-        for grouped, cols in ((by_scalar, slice(0, SHARE)), (by_vector, slice(SHARE, HALF))):
+        for grouped, cols in ((by_vector, slice(SHARE, HALF)), (by_scalar, slice(0, SHARE))):
             nc.vector.quantize_mx(
                 out=q_codes[1][:, cols].bitcast(FP8X4), scales=q_scales[1][:, cols], in_=grouped[:].rearrange("p q j -> p (q j)")
             )

@@ -65,9 +65,9 @@ def tile_attend_plw_silu_topk_kernel(tc, qT, k_words, k_scales, offs, out_0, out
         nc.vector.tensor_copy(dealt_scales[:].rearrange("p (r s) -> p s r", r=PACK), pool_scales[:].indirect(offsets[:]))
         second_raw = shared.tile([P, PACK, HALF], F32, name="second_raw", offset=0, align_bytes=256)
         for rows in (low, high):
-            nc.scalar.dma_start(second_raw[:, rows, :], q_rows[:, rows, HALF:])
+            nc.sync.dma_start(second_raw[:, rows, :], q_rows[:, rows, HALF:])
         for quad in range(4):
-            nc.sync.dma_start(
+            nc.scalar.dma_start(
                 key_scales[32 * quad : 32 * quad + 4, :].bitcast(I32),
                 dealt_scales[PARKED + 4 * quad : PARKED + 4 * quad + 4, :].bitcast(I32),
             )

@@ -93,11 +93,11 @@ def tile_attend_plw_silu_topk_kernel(tc, qT, k_words, k_scales, offs, out_0, out
             out=q_codes[0][:].bitcast(FP8X4), scales=q_scales[0][:], in_=first_grouped[:].rearrange("p q j -> p (q j)")
         )
         by_scalar = rounded.tile([P, SHARE, PACK], BF16, name="by_scalar", offset=2048, align_bytes=256)
-        by_vector = rounded.tile([P, SHARE, PACK], BF16, name="by_vector", offset=0, align_bytes=256)
+        by_vector = rounded.tile([P, SHARE, PACK], BF16, name="by_vector", offset=2560, align_bytes=256)
         interleave(nc.vector.tensor_copy, by_vector[:], second_raw[:, :, SHARE:])
         for rows in (low, high):
             interleave(nc.scalar.copy, by_scalar[:, :, rows], second_raw[:, rows, :SHARE])
-        for grouped, cols in ((by_vector, slice(SHARE, HALF)), (by_scalar, slice(0, SHARE))):
+        for grouped, cols in ((by_scalar, slice(0, SHARE)), (by_vector, slice(SHARE, HALF))):
             nc.vector.quantize_mx(
                 out=q_codes[1][:, cols].bitcast(FP8X4), scales=q_scales[1][:, cols], in_=grouped[:].rearrange("p q j -> p (q j)")
             )

@@ -19,8 +19,8 @@ QUERIES = 256
 HALF = 128
 SHARE = 64
 SCALAR_COLS = 64
+LATE_SCALAR_COLS = 32
 ROWS = 16
-PARKED = P - ROWS
 FLOPS = 2 * 512 * SLOTS * QUERIES
 
 
@@ -33,44 +33,42 @@ def tile_attend_plw_silu_topk_kernel(tc, qT, k_words, k_scales, offs, out_0, out
     halves = QUERIES // HALF
     with ExitStack() as ctx:
         keep = ctx.enter_context(tc.tile_pool(name="keep", bufs=1))
-        shared = ctx.enter_context(tc.tile_pool(name="shared", bufs=1))
         rounded = ctx.enter_context(tc.tile_pool(name="rounded", bufs=1))
         psum = ctx.enter_context(tc.psum_pool(name="psum", bufs=1))
 
         offsets = keep.tile([P, SLOTS // 16], U16, name="offsets")
         pool_words = keep.tile([P, TOKENS], U32, name="pool_words", align_bytes=256)
-        pool_scales = shared.tile([P, TOKENS], U8, name="pool_scales", offset=0, align_bytes=256)
+        pool_scales = keep.tile([P, TOKENS], U8, name="pool_scales", align_bytes=256)
         warm = keep.tile([P, 1], F32, name="warm")
 
         key_scales = keep.tile([P, SLOTS], U8, name="key_scales", align_bytes=256)
 
-        nc.scalar.dma_start(pool_scales[PARKED:, :].bitcast(I32), k_scales[0].bitcast(I32))
+        staged_scales = keep.tile([ROWS, TOKENS], U8, name="staged_scales", align_bytes=256)
+        nc.scalar.dma_start(staged_scales[:].bitcast(I32), k_scales[0].bitcast(I32))
         nc.sync.dma_start(offsets[:], offs)
         word_cols = k_words[0].rearrange("p t r -> p (t r)").bitcast(I32)
         nc.sync.dma_start(pool_words[:].bitcast(I32), word_cols)
         nc.vector.memset(warm[:], 0.0)
         nc.scalar.activation(warm[:], warm[:], SILU)
-        nc.vector.memset(pool_scales[:PARKED, :].bitcast(I32), 0)
+        nc.vector.memset(pool_scales[:].bitcast(I32), 0)
         nc.vector.memset(key_scales[:].bitcast(I32), 0)
+        nc.vector.tensor_copy(pool_scales[:ROWS, :].bitcast(I32), staged_scales[:].bitcast(I32))
         q_rows = qT[0].rearrange("(p j) q -> p j q", j=PACK)
         low, high = slice(0, 2), slice(2, 4)
-        first_raw = []
-        for n, rows in enumerate((low, high)):
-            raw = rounded.tile([P, 2, HALF], F32, name=f"first_raw{n}", offset=1024 * (n + 1), align_bytes=256)
-            nc.sync.dma_start(raw[:], q_rows[:, rows, :HALF])
-            first_raw.append(raw)
+        first_raw = rounded.tile([P, PACK, HALF], F32, name="first_raw", offset=1024, align_bytes=256)
+        nc.sync.dma_start(first_raw[:], q_rows[:, :, :HALF])
 
         dealt_scales = keep.tile([P, SLOTS], U8, name="dealt_scales", align_bytes=256)
         key_words = keep.tile([P, SLOTS], U32, name="key_words", align_bytes=256)
         nc.vector.tensor_copy(dealt_scales[:].rearrange("p (r s) -> p s r", r=PACK), pool_scales[:].indirect(offsets[:]))
-        second_raw = shared.tile([P, PACK, HALF], F32, name="second_raw", offset=0, align_bytes=256)
-        for rows in (low, high):
-            nc.sync.dma_start(second_raw[:, rows, :], q_rows[:, rows, HALF:])
-        for quad in range(4):
+        second_raw = keep.tile([P, PACK, HALF], F32, name="second_raw", align_bytes=256)
+        nc.sync.dma_start(second_raw[:], q_rows[:, :, HALF:])
+        for quad in range(1, 4):
             nc.scalar.dma_start(
                 key_scales[32 * quad : 32 * quad + 4, :].bitcast(I32),
-                dealt_scales[PARKED + 4 * quad : PARKED + 4 * quad + 4, :].bitcast(I32),
+                dealt_scales[4 * quad : 4 * quad + 4, :].bitcast(I32),
             )
+        nc.vector.tensor_copy(key_scales[:4, :].bitcast(I32), dealt_scales[:4, :].bitcast(I32))
         nc.vector.tensor_copy(key_words[:].rearrange("p (r s) -> p s r", r=PACK), pool_words[:].indirect(offsets[:]))
 
         q_codes = [
@@ -79,25 +77,24 @@ def tile_attend_plw_silu_topk_kernel(tc, qT, k_words, k_scales, offs, out_0, out
         ]
         q_scales = [keep.tile([P, HALF], U8, name=f"q_scales{h}", align_bytes=256) for h in range(halves)]
         first_grouped = rounded.tile([P, HALF, PACK], BF16, name="first_grouped", offset=0, align_bytes=256)
-        for rows, raw in zip((low, high), first_raw):
-            interleave(nc.scalar.copy, first_grouped[:, :SCALAR_COLS, rows], raw[:, :, :SCALAR_COLS])
-            nc.gpsimd.tensor_scalar(
-                out=first_grouped[:, SCALAR_COLS:, rows],
-                in0=raw[:, :, SCALAR_COLS:].rearrange("p t c -> p c t"),
-                scalar1=1.0,
-                scalar2=0.0,
-                op0=mybir.AluOpType.mult,
-                op1=mybir.AluOpType.add,
-            )
+        interleave(nc.scalar.copy, first_grouped[:, :SCALAR_COLS, :], first_raw[:, :, :SCALAR_COLS])
+        nc.gpsimd.tensor_scalar(
+            out=first_grouped[:, SCALAR_COLS:, :],
+            in0=first_raw[:, :, SCALAR_COLS:].rearrange("p t c -> p c t"),
+            scalar1=1.0,
+            scalar2=0.0,
+            op0=mybir.AluOpType.mult,
+            op1=mybir.AluOpType.add,
+        )
         nc.vector.quantize_mx(
             out=q_codes[0][:].bitcast(FP8X4), scales=q_scales[0][:], in_=first_grouped[:].rearrange("p q j -> p (q j)")
         )
-        by_scalar = rounded.tile([P, SHARE, PACK], BF16, name="by_scalar", offset=2048, align_bytes=256)
+        by_both = rounded.tile([P, SHARE, PACK], BF16, name="by_both", offset=2048, align_bytes=256)
         by_vector = rounded.tile([P, SHARE, PACK], BF16, name="by_vector", offset=2560, align_bytes=256)
         interleave(nc.vector.tensor_copy, by_vector[:], second_raw[:, :, SHARE:])
-        for rows in (low, high):
-            interleave(nc.scalar.copy, by_scalar[:, :, rows], second_raw[:, rows, :SHARE])
-        for grouped, cols in ((by_scalar, slice(0, SHARE)), (by_vector, slice(SHARE, HALF))):
+        interleave(nc.vector.tensor_copy, by_both[:, LATE_SCALAR_COLS:, :], second_raw[:, :, LATE_SCALAR_COLS:SHARE])
+        interleave(nc.scalar.copy, by_both[:, :LATE_SCALAR_COLS, :], second_raw[:, :, :LATE_SCALAR_COLS])
+        for grouped, cols in ((by_vector, slice(SHARE, HALF)), (by_both, slice(0, SHARE))):
             nc.vector.quantize_mx(
                 out=q_codes[1][:, cols].bitcast(FP8X4), scales=q_scales[1][:, cols], in_=grouped[:].rearrange("p q j -> p (q j)")
             )

@@ -34,6 +34,7 @@ def tile_attend_plw_silu_topk_kernel(tc, qT, k_words, k_scales, offs, out_0, out
     with ExitStack() as ctx:
         keep = ctx.enter_context(tc.tile_pool(name="keep", bufs=1))
         rounded = ctx.enter_context(tc.tile_pool(name="rounded", bufs=1))
+        late = ctx.enter_context(tc.tile_pool(name="late", bufs=1))
         psum = ctx.enter_context(tc.psum_pool(name="psum", bufs=1))
 
         offsets = keep.tile([P, SLOTS // 16], U16, name="offsets")
@@ -50,6 +51,8 @@ def tile_attend_plw_silu_topk_kernel(tc, qT, k_words, k_scales, offs, out_0, out
         nc.sync.dma_start(pool_words[:].bitcast(I32), word_cols)
         nc.vector.memset(warm[:], 0.0)
         nc.scalar.activation(warm[:], warm[:], SILU)
+        zero_bias = late.tile([P, 1], F32, name="zero_bias", offset=0, align_bytes=256)
+        nc.vector.memset(zero_bias[:], 0.0)
         nc.vector.memset(pool_scales[:].bitcast(I32), 0)
         nc.vector.memset(key_scales[:].bitcast(I32), 0)
         nc.vector.tensor_copy(pool_scales[:ROWS, :].bitcast(I32), staged_scales[:].bitcast(I32))
@@ -100,42 +103,56 @@ def tile_attend_plw_silu_topk_kernel(tc, qT, k_words, k_scales, offs, out_0, out
             )
 
         y_codes = keep.tile([P, QUERIES], U32, name="y_codes", align_bytes=256)
-        y_scales = keep.tile([P, QUERIES], U8, name="y_scales", align_bytes=256)
         y = keep.tile([P, PACK, QUERIES], F32, name="y", align_bytes=256)
         y_rows = out_0.rearrange("(p r) q -> p r q", r=PACK)
         word_rows = out_1[0].rearrange("p q u -> p (q u)").bitcast(I32)
         pair_order = [[low, high], [high, low]]
+        grouped_halves = []
         for h in range(halves):
             cols = slice(h * HALF, (h + 1) * HALF)
             y_grouped = keep.tile([P, HALF, PACK], BF16, name=f"y_grouped{h}", align_bytes=256)
+            last_half = h == halves - 1
             for n, places in enumerate(pair_order[h]):
-                bank = psum.tile([P, 2, HALF], F32, name=f"bank{h}{n}")
-                for e in range(2):
-                    r = places.start + e
-                    keys = slice(r * P, (r + 1) * P)
-                    nc.tensor.matmul_mx(
-                        out=bank[:, e, :],
-                        lhsT=key_words[:, keys].bitcast(FP8X4),
-                        lhsT_scale=key_scales[:, keys],
-                        rhs=q_codes[h][:].bitcast(FP8X4),
-                        rhs_scale=q_scales[h][:],
-                        start=True,
-                        stop=True,
-                    )
-                if (h, n) == (halves - 1, 1):
-                    nc.scalar.activation(y_grouped[:, :, places], bank[:].rearrange("p e q -> p q e"), SILU)
-                    nc.scalar.activation(y[:, places, cols], bank[:], SILU)
-                else:
-                    nc.scalar.activation(y[:, places, cols], bank[:], SILU)
+                last_pair = last_half and n == 1
+                single = last_half and n == 0
+                groups = [[places.start], [places.start + 1]] if single else [[places.start, places.start + 1]]
+                for group in groups:
+                    bank = psum.tile([P, len(group), HALF], F32, name=f"bank{h}{group[0]}")
+                    for e, r in enumerate(group):
+                        keys = slice(r * P, (r + 1) * P)
+                        nc.tensor.matmul_mx(
+                            out=bank[:, e, :],
+                            lhsT=key_words[:, keys].bitcast(FP8X4),
+                            lhsT_scale=key_scales[:, keys],
+                            rhs=q_codes[h][:].bitcast(FP8X4),
+                            rhs_scale=q_scales[h][:],
+                            start=True,
+                            stop=True,
+                        )
+                    rows = slice(group[0], group[-1] + 1)
+                    if last_pair:
+                        once, twice = slice(0, SHARE), slice(SHARE, HALF)
+                        y_half = y[:, rows, cols]
+                        nc.scalar.activation(y_half[:, :, once], bank[:, :, once], SILU, bias=zero_bias[:])
+                        nc.scalar.activation(y_grouped[:, twice, rows], bank[:, :, twice].rearrange("p e q -> p q e"), SILU)
+                        nc.scalar.activation(y_half[:, :, twice], bank[:, :, twice], SILU)
+                        interleave(nc.vector.tensor_copy, y_grouped[:, once, rows], y_half[:, :, once])
+                    else:
+                        nc.scalar.activation(y[:, rows, cols], bank[:], SILU)
+                if not last_pair:
                     interleave(nc.vector.tensor_copy, y_grouped[:, :, places], y[:, places, cols])
                 if places == low:
                     nc.sync.dma_start(y_rows[:, low, cols], y[:, low, cols])
-                elif h == halves - 1:
+                elif last_half:
                     nc.sync.dma_start(y_rows[:, high, :], y[:, high, :])
+            grouped_halves.append(y_grouped)
+        y_scales = late.tile([P, QUERIES], U8, name="y_scales", offset=0, align_bytes=256)
+        for h, c0, c1 in ((0, 0, HALF), (1, SHARE, HALF), (1, 0, SHARE)):
+            part = slice(h * HALF + c0, h * HALF + c1)
             nc.vector.quantize_mx(
-                out=y_codes[:, cols].bitcast(FP8X4),
-                scales=y_scales[:, cols],
-                in_=y_grouped[:].rearrange("p q r -> p (q r)"),
+                out=y_codes[:, part].bitcast(FP8X4),
+                scales=y_scales[:, part],
+                in_=grouped_halves[h][:, c0:c1, :].rearrange("p q r -> p (q r)"),
             )
         nc.sync.dma_start(word_rows, y_codes[:].bitcast(I32))
         for quad in range(4):

@@ -89,9 +89,12 @@ def tile_attend_plw_silu_topk_kernel(tc, qT, k_words, k_scales, offs, out_0, out
             op0=mybir.AluOpType.mult,
             op1=mybir.AluOpType.add,
         )
-        nc.vector.quantize_mx(
-            out=q_codes[0][:].bitcast(FP8X4), scales=q_scales[0][:], in_=first_grouped[:].rearrange("p q j -> p (q j)")
-        )
+        for cols in (slice(0, SCALAR_COLS), slice(SCALAR_COLS, HALF)):
+            nc.vector.quantize_mx(
+                out=q_codes[0][:, cols].bitcast(FP8X4),
+                scales=q_scales[0][:, cols],
+                in_=first_grouped[:, cols, :].rearrange("p q j -> p (q j)"),
+            )
         by_both = rounded.tile([P, SHARE, PACK], BF16, name="by_both", offset=2048, align_bytes=256)
         by_vector = rounded.tile([P, SHARE, PACK], BF16, name="by_vector", offset=2560, align_bytes=256)
         interleave(nc.vector.tensor_copy, by_vector[:], second_raw[:, :, SHARE:])
@@ -114,7 +117,7 @@ def tile_attend_plw_silu_topk_kernel(tc, qT, k_words, k_scales, offs, out_0, out
             last_half = h == halves - 1
             for n, places in enumerate(pair_order[h]):
                 last_pair = last_half and n == 1
-                single = last_half and n == 0
+                single = not last_pair
                 groups = [[places.start], [places.start + 1]] if single else [[places.start, places.start + 1]]
                 for group in groups:
                     bank = psum.tile([P, len(group), HALF], F32, name=f"bank{h}{group[0]}")

from contextlib import ExitStack

import concourse.mybir as mybir

F32 = mybir.dt.float32
BF16 = mybir.dt.bfloat16
I32 = mybir.dt.int32
U32 = mybir.dt.uint32
U16 = mybir.dt.uint16
U8 = mybir.dt.uint8
FP8X4 = mybir.dt.float8_e4m3fn_x4
SILU = mybir.ActivationFunctionType.Silu

P = 128
PACK = 4
SLOTS = 512
TOKENS = 2048
QUERIES = 256
HALF = 128
SHARE = 64
SCALAR_COLS = 64
LATE_SCALAR_COLS = 32
ROWS = 16
FLOPS = 2 * 512 * SLOTS * QUERIES


def interleave(copy, dst, src):
    copy(out=dst.rearrange("p (c i) t -> p c t i", i=4), in_=src.rearrange("p t (c i) -> p c t i", i=4))


def tile_attend_plw_silu_topk_kernel(tc, qT, k_words, k_scales, offs, out_0, out_1, out_2):
    nc = tc.nc
    halves = QUERIES // HALF
    with ExitStack() as ctx:
        keep = ctx.enter_context(tc.tile_pool(name="keep", bufs=1))
        rounded = ctx.enter_context(tc.tile_pool(name="rounded", bufs=1))
        late = ctx.enter_context(tc.tile_pool(name="late", bufs=1))
        psum = ctx.enter_context(tc.psum_pool(name="psum", bufs=1))

        offsets = keep.tile([P, SLOTS // 16], U16, name="offsets")
        pool_words = keep.tile([P, TOKENS], U32, name="pool_words", align_bytes=256)
        pool_scales = keep.tile([P, TOKENS], U8, name="pool_scales", align_bytes=256)
        warm = keep.tile([P, 1], F32, name="warm")

        key_scales = keep.tile([P, SLOTS], U8, name="key_scales", align_bytes=256)

        staged_scales = keep.tile([ROWS, TOKENS], U8, name="staged_scales", align_bytes=256)
        nc.scalar.dma_start(staged_scales[:].bitcast(I32), k_scales[0].bitcast(I32))
        nc.sync.dma_start(offsets[:], offs)
        word_cols = k_words[0].rearrange("p t r -> p (t r)").bitcast(I32)
        nc.sync.dma_start(pool_words[:].bitcast(I32), word_cols)
        nc.vector.memset(warm[:], 0.0)
        nc.scalar.activation(warm[:], warm[:], SILU)
        zero_bias = late.tile([P, 1], F32, name="zero_bias", offset=0, align_bytes=256)
        nc.vector.memset(zero_bias[:], 0.0)
        nc.vector.memset(pool_scales[:].bitcast(I32), 0)
        nc.vector.memset(key_scales[:].bitcast(I32), 0)
        nc.vector.tensor_copy(pool_scales[:ROWS, :].bitcast(I32), staged_scales[:].bitcast(I32))
        q_rows = qT[0].rearrange("(p j) q -> p j q", j=PACK)
        low, high = slice(0, 2), slice(2, 4)
        first_raw = rounded.tile([P, PACK, HALF], F32, name="first_raw", offset=1024, align_bytes=256)
        nc.sync.dma_start(first_raw[:], q_rows[:, :, :HALF])

        dealt_scales = keep.tile([P, SLOTS], U8, name="dealt_scales", align_bytes=256)
        key_words = keep.tile([P, SLOTS], U32, name="key_words", align_bytes=256)
        nc.vector.tensor_copy(dealt_scales[:].rearrange("p (r s) -> p s r", r=PACK), pool_scales[:].indirect(offsets[:]))
        second_raw = keep.tile([P, PACK, HALF], F32, name="second_raw", align_bytes=256)
        nc.sync.dma_start(second_raw[:], q_rows[:, :, HALF:])
        for quad in range(1, 4):
            nc.scalar.dma_start(
                key_scales[32 * quad : 32 * quad + 4, :].bitcast(I32),
                dealt_scales[4 * quad : 4 * quad + 4, :].bitcast(I32),
            )
        nc.vector.tensor_copy(key_scales[:4, :].bitcast(I32), dealt_scales[:4, :].bitcast(I32))
        nc.vector.tensor_copy(key_words[:].rearrange("p (r s) -> p s r", r=PACK), pool_words[:].indirect(offsets[:]))

        q_codes = [
            keep.tile([P, HALF], U32, name="q_codes0", align_bytes=256),
            rounded.tile([P, HALF], U32, name="q_codes1", offset=SHARE * PACK * 2, align_bytes=256),
        ]
        q_scales = [keep.tile([P, HALF], U8, name=f"q_scales{h}", align_bytes=256) for h in range(halves)]
        first_grouped = rounded.tile([P, HALF, PACK], BF16, name="first_grouped", offset=0, align_bytes=256)
        interleave(nc.scalar.copy, first_grouped[:, :SCALAR_COLS, :], first_raw[:, :, :SCALAR_COLS])
        nc.gpsimd.tensor_scalar(
            out=first_grouped[:, SCALAR_COLS:, :],
            in0=first_raw[:, :, SCALAR_COLS:].rearrange("p t c -> p c t"),
            scalar1=1.0,
            scalar2=0.0,
            op0=mybir.AluOpType.mult,
            op1=mybir.AluOpType.add,
        )
        for cols in (slice(0, SCALAR_COLS), slice(SCALAR_COLS, HALF)):
            nc.vector.quantize_mx(
                out=q_codes[0][:, cols].bitcast(FP8X4),
                scales=q_scales[0][:, cols],
                in_=first_grouped[:, cols, :].rearrange("p q j -> p (q j)"),
            )
        by_both = rounded.tile([P, SHARE, PACK], BF16, name="by_both", offset=2048, align_bytes=256)
        by_vector = rounded.tile([P, SHARE, PACK], BF16, name="by_vector", offset=2560, align_bytes=256)
        interleave(nc.vector.tensor_copy, by_vector[:], second_raw[:, :, SHARE:])
        interleave(nc.vector.tensor_copy, by_both[:, LATE_SCALAR_COLS:, :], second_raw[:, :, LATE_SCALAR_COLS:SHARE])
        interleave(nc.scalar.copy, by_both[:, :LATE_SCALAR_COLS, :], second_raw[:, :, :LATE_SCALAR_COLS])
        for grouped, cols in ((by_vector, slice(SHARE, HALF)), (by_both, slice(0, SHARE))):
            nc.vector.quantize_mx(
                out=q_codes[1][:, cols].bitcast(FP8X4), scales=q_scales[1][:, cols], in_=grouped[:].rearrange("p q j -> p (q j)")
            )

        y_codes = keep.tile([P, QUERIES], U32, name="y_codes", align_bytes=256)
        y = keep.tile([P, PACK, QUERIES], F32, name="y", align_bytes=256)
        y_rows = out_0.rearrange("(p r) q -> p r q", r=PACK)
        word_rows = out_1[0].rearrange("p q u -> p (q u)").bitcast(I32)
        pair_order = [[low, high], [high, low]]
        grouped_halves = []
        for h in range(halves):
            cols = slice(h * HALF, (h + 1) * HALF)
            y_grouped = keep.tile([P, HALF, PACK], BF16, name=f"y_grouped{h}", align_bytes=256)
            last_half = h == halves - 1
            for n, places in enumerate(pair_order[h]):
                last_pair = last_half and n == 1
                single = not last_pair
                groups = [[places.start], [places.start + 1]] if single else [[places.start, places.start + 1]]
                for group in groups:
                    bank = psum.tile([P, len(group), HALF], F32, name=f"bank{h}{group[0]}")
                    for e, r in enumerate(group):
                        keys = slice(r * P, (r + 1) * P)
                        nc.tensor.matmul_mx(
                            out=bank[:, e, :],
                            lhsT=key_words[:, keys].bitcast(FP8X4),
                            lhsT_scale=key_scales[:, keys],
                            rhs=q_codes[h][:].bitcast(FP8X4),
                            rhs_scale=q_scales[h][:],
                            start=True,
                            stop=True,
                        )
                    rows = slice(group[0], group[-1] + 1)
                    if last_pair:
                        once, twice = slice(0, SHARE), slice(SHARE, HALF)
                        y_half = y[:, rows, cols]
                        nc.scalar.activation(y_half[:, :, once], bank[:, :, once], SILU, bias=zero_bias[:])
                        nc.scalar.activation(y_grouped[:, twice, rows], bank[:, :, twice].rearrange("p e q -> p q e"), SILU)
                        nc.scalar.activation(y_half[:, :, twice], bank[:, :, twice], SILU)
                        interleave(nc.vector.tensor_copy, y_grouped[:, once, rows], y_half[:, :, once])
                    else:
                        nc.scalar.activation(y[:, rows, cols], bank[:], SILU)
                if not last_pair:
                    interleave(nc.vector.tensor_copy, y_grouped[:, :, places], y[:, places, cols])
                if places == low:
                    nc.sync.dma_start(y_rows[:, low, cols], y[:, low, cols])
                elif last_half:
                    nc.sync.dma_start(y_rows[:, high, :], y[:, high, :])
            grouped_halves.append(y_grouped)
        y_scales = late.tile([P, QUERIES], U8, name="y_scales", offset=0, align_bytes=256)
        for h, c0, c1 in ((0, 0, HALF), (1, SHARE, HALF), (1, 0, SHARE)):
            part = slice(h * HALF + c0, h * HALF + c1)
            nc.vector.quantize_mx(
                out=y_codes[:, part].bitcast(FP8X4),
                scales=y_scales[:, part],
                in_=grouped_halves[h][:, c0:c1, :].rearrange("p q r -> p (q r)"),
            )
        nc.sync.dma_start(word_rows, y_codes[:].bitcast(I32))
        for quad in range(4):
            queue = nc.scalar if quad < 3 else nc.sync
            queue.dma_start(
                out_2[0, 4 * quad : 4 * quad + 4, :].bitcast(I32),
                y_scales[32 * quad : 32 * quad + 4, :].bitcast(I32),
            )
